import numpy as np
import ml_dtypes


def mxq(x, axis, fmt="e4m3"):
    dtype, down = {"e4m3": (ml_dtypes.float8_e4m3fn, 7), "e5m2": (ml_dtypes.float8_e5m2, 14)}[fmt]
    v = np.moveaxis(np.asarray(x, np.float32).astype(ml_dtypes.bfloat16).astype(np.float64), axis, -1)
    blocks = v.reshape(v.shape[:-1] + (-1, 32))
    amax = np.abs(blocks).max(-1, keepdims=True)
    byte = np.maximum(np.where(amax > 0, np.frexp(amax)[1] - 1 + 127, 0) - down, 1)
    scale = np.exp2(byte - 127.0)
    codes = (blocks / scale).astype(np.float32).astype(dtype).astype(np.float64)
    return np.moveaxis((codes * scale).reshape(v.shape), -1, axis)


WIDE = False


def mx_kscale(k, group=512):
    if not WIDE:
        return np.ones(k)
    levels = np.array([10, -10, 5, -5, 0])
    if group != 512:
        return np.exp2(np.random.permutation(np.resize(levels, k // group))).repeat(group)
    if k % 512:
        return np.exp2(np.random.permutation(np.resize(levels, k // 32))).repeat(32)
    a = np.empty((k // 512, 16))
    for p in range(k // 512):
        a[p, :8] = np.random.permutation(np.resize(levels, 8))
        for g in range(8):
            far = levels[np.abs(levels - a[p, g]) >= 10]
            a[p, g + 8] = far[np.random.randint(len(far))]
    return np.exp2(a.ravel()).repeat(32)


def f64(x):
    return np.asarray(x).astype(np.float64)


def sigmoid(v):
    return 1.0 / (1.0 + np.exp(-v))


G, D, M, O, N = 2, 256, 128, 256, 512


def setup_inputs():
    n = np.random.standard_normal
    s_d = mx_kscale(D, 0)
    s_o = mx_kscale(O, 0)
    return {
        "x": (n((G, D, N)) * s_d[:, None]).astype(np.float32),
        "w1": (n((G, D, M)) / np.sqrt(D) / s_d[:, None]).astype(np.float32),
        "w2": (n((G, D, M)) / np.sqrt(D) / s_d[:, None]).astype(np.float32),
        "tp": (np.random.uniform(0.5, 1.2, (G, M, 1))).astype(np.float32),
        "wo": (n((G, O, M)) / np.sqrt(O) / s_o[:, None]).astype(np.float32),
        "dy": (n((G, O, N)) * s_o[:, None]).astype(np.float32),
        "dx": (n((G, D, N)) * s_d[:, None]).astype(np.float32),
        "og": (np.random.uniform(0.5, 2.0, (G, M, 1))).astype(np.float32),
        "base": (0.3 * n((G, M, N))).astype(np.float32),
    }


def reference(x, w1, w2, tp, wo, dy, dx, og, base):
    w1q = mxq(f64(w1), 1, "e4m3")
    xq = mxq(f64(x), 1, "e4m3")
    z1 = w1q.transpose(0, 2, 1) @ xq
    dxq = mxq(f64(dx), 1, "e4m3")
    tz1 = w1q.transpose(0, 2, 1) @ dxq
    w2q = mxq(f64(w2), 1, "e4m3")
    z2 = w2q.transpose(0, 2, 1) @ xq
    tz2 = w2q.transpose(0, 2, 1) @ dxq
    s1 = z1 * f64(tp)
    woq = mxq(f64(wo), 1, "e4m3")
    dyq = mxq(f64(dy), 1, "e4m3")
    c0 = woq.transpose(0, 2, 1) @ dyq
    dls = np.sum(c0 * sigmoid(z2) * (-1.0), axis=-1, keepdims=True)
    xs1 = tz1 * f64(tp)
    xdls = np.sum(tz2 * sigmoid(z2) * (1.0 - sigmoid(z2)) * c0 * (-1.0), axis=-1, keepdims=True)
    xds1 = tz2 * sigmoid(z2) * (1.0 - sigmoid(z2)) * c0 + (xdls - np.sum(xs1 * np.exp(s1), axis=-1, keepdims=True) * dls / np.sum(np.exp(s1), axis=-1, keepdims=True)) / np.sum(np.exp(s1), axis=-1, keepdims=True) * np.exp(s1) + xs1 * np.exp(s1) * dls / np.sum(np.exp(s1), axis=-1, keepdims=True)
    xdz1 = xds1 * f64(tp)
    y = xdz1 * f64(og) + f64(base)
    return y

@@ -1,0 +1,215 @@
+from contextlib import ExitStack
+
+import concourse.mybir as mybir
+
+G, D, M, N = 2, 256, 128, 512
+
+F32 = mybir.dt.float32
+BF16 = mybir.dt.bfloat16
+U32 = mybir.dt.uint32
+U8 = mybir.dt.uint8
+FP8X4 = mybir.dt.float8_e4m3fn_x4
+ALU = mybir.AluOpType
+ACT = mybir.ActivationFunctionType
+
+P = 128
+PACK = 4
+ROWS = D // PACK
+RUN = 4
+
+FLOPS = 5 * 2 * G * D * M * N
+
+X_VECTOR_COLS = 344
+DY_VECTOR_COLS = 384
+DX_VECTOR_COLS = 64
+
+
+def tile_rows_hvrowlog_kernel(tc, x, w1, w2, tp, wo, dy, dx, og, base, out):
+    nc = tc.nc
+
+    with ExitStack() as ctx:
+        sb = ctx.enter_context(tc.tile_pool(name="sb", bufs=1))
+        ps = ctx.enter_context(tc.psum_pool(name="ps", bufs=1))
+        ctx.enter_context(tc.manual_schedule())
+
+        def load_operand(name, src):
+            width = src.shape[2]
+            raw = sb.tile([P, PACK, width], F32, name=name + "raw", align_bytes=64)
+            nc.sync.dma_start(out=raw[:], in_=src.rearrange("g (p j) c -> (g p) j c", j=PACK))
+            return {
+                "raw": raw,
+                "packed": sb.tile([P, width, PACK], BF16, name=name + "packed", align_bytes=64),
+                "codes": sb.tile([P, width], U32, name=name + "codes", align_bytes=64),
+                "scales": sb.tile([P, width], U8, name=name + "scales", align_bytes=64),
+                "width": width,
+            }
+
+        def interleave(copy, operand, first, last):
+            copy(
+                out=operand["packed"][:, first:last, :].rearrange("p (c i) j -> p c j i", i=RUN),
+                in_=operand["raw"][:, :, first:last].rearrange("p j (c i) -> p c j i", i=RUN),
+            )
+
+        def quantise(operand):
+            nc.vector.quantize_mx(
+                out=operand["codes"][:].bitcast(FP8X4),
+                scales=operand["scales"][:],
+                in_=operand["packed"][:].rearrange("p c j -> p (c j)"),
+            )
+
+        def product(bank, weights, moving):
+            for g in range(G):
+                rows = slice(ROWS * g, ROWS * (g + 1))
+                nc.tensor.matmul_mx(
+                    out=bank[g][:],
+                    lhsT=weights["codes"][rows, :].bitcast(FP8X4),
+                    lhsT_scale=weights["scales"][rows, :],
+                    rhs=moving["codes"][rows, :].bitcast(FP8X4),
+                    rhs_scale=moving["scales"][rows, :],
+                    start=True,
+                    stop=True,
+                )
+
+        def per_group(pool, name, width):
+            return [pool.tile([P, width], F32, name="%s%d" % (name, g)) for g in range(G)]
+
+        def column(stat, g):
+            return stat[:, g : g + 1]
+
+        on_vector = nc.vector.tensor_copy
+        on_scalar = nc.scalar.copy
+
+        xq = load_operand("x", x)
+        w2q = load_operand("w2", w2)
+        w1q = load_operand("w1", w1)
+        woq = load_operand("wo", wo)
+        dyq = load_operand("dy", dy)
+        dxq = load_operand("dx", dx)
+        base_sb = sb.tile([P, G, N], F32)
+        nc.sync.dma_start(out=base_sb[:], in_=base.rearrange("g m n -> m g n"))
+        temper = sb.tile([P, G], F32)
+        gain = sb.tile([P, G], F32)
+        with nc.allow_non_contiguous_dma(reason="one value per feature, features on partitions"):
+            nc.scalar.dma_start(out=temper[:], in_=tp.rearrange("g m o -> m (g o)"))
+            nc.scalar.dma_start(out=gain[:], in_=og.rearrange("g m o -> m (g o)"))
+
+        z2_then_tz1 = per_group(ps, "bank_a", N)
+        z1 = per_group(ps, "bank_b", N)
+        c0 = per_group(ps, "bank_c", N)
+        tz2 = per_group(ps, "bank_d", N)
+
+        th = per_group(sb, "th", N)
+        ex = per_group(sb, "ex", N)
+        gate = per_group(sb, "gate", N)
+        neg_a = per_group(sb, "neg_a", N)
+        neg_w = per_group(sb, "neg_w", N)
+        result = per_group(sb, "result", N)
+
+        quarter_k = sb.tile([P, G], F32)
+        half_k_temper = sb.tile([P, G], F32)
+        exp_sum = sb.tile([P, G], F32)
+        inv_sum = sb.tile([P, G], F32)
+        w_factor = sb.tile([P, G], F32)
+        gate_sum = sb.tile([P, G], F32)
+        w_scale = sb.tile([P, G], F32)
+        neg_a_sum = sb.tile([P, G], F32)
+        neg_w_sum = sb.tile([P, G], F32)
+        share_scale = sb.tile([P, G], F32)
+
+        interleave(on_vector, xq, 0, X_VECTOR_COLS)
+        interleave(on_scalar, xq, X_VECTOR_COLS, N)
+        interleave(on_vector, w2q, 0, M)
+        nc.vector.scalar_tensor_tensor(
+            out=quarter_k[:], in0=temper[:], scalar=0.25, in1=gain[:], op0=ALU.mult, op1=ALU.mult
+        )
+        interleave(on_scalar, w1q, 0, M)
+        interleave(on_scalar, woq, 0, M)
+        quantise(xq)
+        quantise(w2q)
+        product(z2_then_tz1, w2q, xq)
+        quantise(w1q)
+        product(z1, w1q, xq)
+        nc.vector.scalar_tensor_tensor(
+            out=half_k_temper[:], in0=quarter_k[:], scalar=2.0, in1=temper[:], op0=ALU.mult, op1=ALU.mult
+        )
+        quantise(woq)
+
+        for g in range(G):
+            nc.scalar.activation(out=th[g][:], in_=z2_then_tz1[g][:], func=ACT.Tanh, scale=0.5)
+
+        interleave(on_vector, dyq, 0, DY_VECTOR_COLS)
+        interleave(on_scalar, dyq, DY_VECTOR_COLS, N)
+        quantise(dyq)
+        product(c0, woq, dyq)
+
+        for g in range(G):
+            nc.scalar.activation(
+                out=ex[g][:], in_=z1[g][:], func=ACT.Exp, scale=column(temper, g), accum_out=column(exp_sum, g)
+            )
+        interleave(on_scalar, dxq, DX_VECTOR_COLS, N)
+
+        nc.vector.reciprocal(out=inv_sum[:], in_=exp_sum[:])
+        for g in range(G):
+            nc.vector.scalar_tensor_tensor(
+                out=gate[g][:], in0=th[g][:], scalar=1.0, in1=c0[g][:], op0=ALU.add, op1=ALU.mult,
+                accum_out=column(gate_sum, g),
+            )
+        nc.vector.tensor_tensor(out=w_factor[:], in0=inv_sum[:], in1=half_k_temper[:], op=ALU.mult)
+        interleave(on_vector, dxq, 0, DX_VECTOR_COLS)
+
+        def finish_gate(g):
+            nc.vector.scalar_tensor_tensor(
+                out=gate[g][:], in0=th[g][:], scalar=1.0, in1=gate[g][:], op0=ALU.subtract, op1=ALU.mult
+            )
+
+        finish_gate(0)
+        quantise(dxq)
+        product(tz2, w2q, dxq)
+        product(z2_then_tz1, w1q, dxq)
+        nc.vector.tensor_tensor(out=w_scale[:], in0=gate_sum[:], in1=w_factor[:], op=ALU.mult)
+        finish_gate(1)
+
+        def gate_term(g):
+            nc.vector.scalar_tensor_tensor(
+                out=neg_a[g][:], in0=tz2[g][:], scalar=column(quarter_k, g), in1=gate[g][:],
+                op0=ALU.mult, op1=ALU.mult, accum_out=column(neg_a_sum, g),
+            )
+
+        def share_term(g):
+            nc.vector.scalar_tensor_tensor(
+                out=neg_w[g][:], in0=z2_then_tz1[g][:], scalar=column(w_scale, g), in1=ex[g][:],
+                op0=ALU.mult, op1=ALU.mult, accum_out=column(neg_w_sum, g),
+            )
+
+        def row_correction(g):
+            nc.vector.tensor_scalar(
+                out=column(share_scale, g), in0=column(neg_a_sum, g), scalar1=column(neg_w_sum, g),
+                scalar2=column(inv_sum, g), op0=ALU.add, op1=ALU.mult,
+            )
+
+        def subtract(g, minuend, term, cols):
+            nc.vector.tensor_tensor(out=result[g][:, cols], in0=minuend, in1=term[g][:, cols], op=ALU.subtract)
+
+        def finish(g, cols):
+            nc.vector.scalar_tensor_tensor(
+                out=result[g][:, cols], in0=ex[g][:, cols], scalar=column(share_scale, g), in1=result[g][:, cols],
+                op0=ALU.mult, op1=ALU.add,
+            )
+            nc.sync.dma_start(out=out[g, :, cols], in_=result[g][:, cols])
+
+        whole = slice(0, N)
+        halves = [slice(0, N // 2), slice(N // 2, N)]
+        gate_term(0)
+        share_term(0)
+        gate_term(1)
+        subtract(0, base_sb[:, 0, :], neg_a, whole)
+        share_term(1)
+        row_correction(0)
+        subtract(0, result[0][:], neg_w, whole)
+        subtract(1, base_sb[:, 1, :], neg_a, whole)
+        finish(0, whole)
+        row_correction(1)
+        for cols in halves:
+            subtract(1, result[1][:, cols], neg_w, cols)
+        for cols in halves:
+            finish(1, cols)

@@ -20,8 +20,8 @@ RUN = 4
 FLOPS = 5 * 2 * G * D * M * N
 
 X_VECTOR_COLS = 344
-DY_VECTOR_COLS = 384
-DX_VECTOR_COLS = 64
+DY_VECTOR_COLS = 400
+DX_VECTOR_COLS = 152
 
 
 def tile_rows_hvrowlog_kernel(tc, x, w1, w2, tp, wo, dy, dx, og, base, out):
@@ -81,17 +81,17 @@ def tile_rows_hvrowlog_kernel(tc, x, w1, w2, tp, wo, dy, dx, og, base, out):
 
         xq = load_operand("x", x)
         w2q = load_operand("w2", w2)
-        w1q = load_operand("w1", w1)
-        woq = load_operand("wo", wo)
         dyq = load_operand("dy", dy)
+        woq = load_operand("wo", wo)
+        w1q = load_operand("w1", w1)
         dxq = load_operand("dx", dx)
-        base_sb = sb.tile([P, G, N], F32)
-        nc.sync.dma_start(out=base_sb[:], in_=base.rearrange("g m n -> m g n"))
         temper = sb.tile([P, G], F32)
         gain = sb.tile([P, G], F32)
         with nc.allow_non_contiguous_dma(reason="one value per feature, features on partitions"):
-            nc.scalar.dma_start(out=temper[:], in_=tp.rearrange("g m o -> m (g o)"))
-            nc.scalar.dma_start(out=gain[:], in_=og.rearrange("g m o -> m (g o)"))
+            nc.sync.dma_start(out=temper[:], in_=tp.rearrange("g m o -> m (g o)"))
+            nc.sync.dma_start(out=gain[:], in_=og.rearrange("g m o -> m (g o)"))
+        base_sb = sb.tile([P, G, N], F32)
+        nc.sync.dma_start(out=base_sb[:], in_=base.rearrange("g m n -> m g n"))
 
         z2_then_tz1 = per_group(ps, "bank_a", N)
         z1 = per_group(ps, "bank_b", N)
@@ -109,52 +109,49 @@ def tile_rows_hvrowlog_kernel(tc, x, w1, w2, tp, wo, dy, dx, og, base, out):
         half_k_temper = sb.tile([P, G], F32)
         exp_sum = sb.tile([P, G], F32)
         inv_sum = sb.tile([P, G], F32)
-        w_factor = sb.tile([P, G], F32)
         gate_sum = sb.tile([P, G], F32)
+        scaled_gate_sum = sb.tile([P, G], F32)
         w_scale = sb.tile([P, G], F32)
         neg_a_sum = sb.tile([P, G], F32)
+        neg_a_mean = sb.tile([P, G], F32)
         neg_w_sum = sb.tile([P, G], F32)
         share_scale = sb.tile([P, G], F32)
+
+        def times(dst, src, factor, g):
+            nc.scalar.activation(out=column(dst, g), in_=column(src, g), func=ACT.Copy, scale=column(factor, g))
 
         interleave(on_vector, xq, 0, X_VECTOR_COLS)
         interleave(on_scalar, xq, X_VECTOR_COLS, N)
         interleave(on_vector, w2q, 0, M)
-        nc.vector.scalar_tensor_tensor(
-            out=quarter_k[:], in0=temper[:], scalar=0.25, in1=gain[:], op0=ALU.mult, op1=ALU.mult
-        )
-        interleave(on_scalar, w1q, 0, M)
-        interleave(on_scalar, woq, 0, M)
         quantise(xq)
         quantise(w2q)
         product(z2_then_tz1, w2q, xq)
-        quantise(w1q)
-        product(z1, w1q, xq)
-        nc.vector.scalar_tensor_tensor(
-            out=half_k_temper[:], in0=quarter_k[:], scalar=2.0, in1=temper[:], op0=ALU.mult, op1=ALU.mult
-        )
-        quantise(woq)
-
-        for g in range(G):
-            nc.scalar.activation(out=th[g][:], in_=z2_then_tz1[g][:], func=ACT.Tanh, scale=0.5)
 
         interleave(on_vector, dyq, 0, DY_VECTOR_COLS)
         interleave(on_scalar, dyq, DY_VECTOR_COLS, N)
+        interleave(on_scalar, woq, 0, M)
+        quantise(woq)
         quantise(dyq)
         product(c0, woq, dyq)
 
         for g in range(G):
+            nc.scalar.activation(out=th[g][:], in_=z2_then_tz1[g][:], func=ACT.Tanh, scale=0.5)
+
+        interleave(on_vector, w1q, 0, M)
+        quantise(w1q)
+        product(z1, w1q, xq)
+
+        interleave(on_scalar, dxq, DX_VECTOR_COLS, N)
+        for g in range(G):
             nc.scalar.activation(
                 out=ex[g][:], in_=z1[g][:], func=ACT.Exp, scale=column(temper, g), accum_out=column(exp_sum, g)
             )
-        interleave(on_scalar, dxq, DX_VECTOR_COLS, N)
 
-        nc.vector.reciprocal(out=inv_sum[:], in_=exp_sum[:])
         for g in range(G):
             nc.vector.scalar_tensor_tensor(
                 out=gate[g][:], in0=th[g][:], scalar=1.0, in1=c0[g][:], op0=ALU.add, op1=ALU.mult,
                 accum_out=column(gate_sum, g),
             )
-        nc.vector.tensor_tensor(out=w_factor[:], in0=inv_sum[:], in1=half_k_temper[:], op=ALU.mult)
         interleave(on_vector, dxq, 0, DX_VECTOR_COLS)
 
         def finish_gate(g):
@@ -166,29 +163,41 @@ def tile_rows_hvrowlog_kernel(tc, x, w1, w2, tp, wo, dy, dx, og, base, out):
         quantise(dxq)
         product(tz2, w2q, dxq)
         product(z2_then_tz1, w1q, dxq)
-        nc.vector.tensor_tensor(out=w_scale[:], in0=gate_sum[:], in1=w_factor[:], op=ALU.mult)
+        nc.vector.scalar_tensor_tensor(
+            out=quarter_k[:], in0=temper[:], scalar=0.25, in1=gain[:], op0=ALU.mult, op1=ALU.mult
+        )
         finish_gate(1)
+        nc.vector.scalar_tensor_tensor(
+            out=half_k_temper[:], in0=quarter_k[:], scalar=2.0, in1=temper[:], op0=ALU.mult, op1=ALU.mult
+        )
+        nc.vector.reciprocal(out=inv_sum[:], in_=exp_sum[:])
+        for g in range(G):
+            times(scaled_gate_sum, gate_sum, half_k_temper, g)
+        for g in range(G):
+            times(w_scale, scaled_gate_sum, inv_sum, g)
 
-        def gate_term(g):
+        for g in range(G):
             nc.vector.scalar_tensor_tensor(
                 out=neg_a[g][:], in0=tz2[g][:], scalar=column(quarter_k, g), in1=gate[g][:],
                 op0=ALU.mult, op1=ALU.mult, accum_out=column(neg_a_sum, g),
             )
+            nc.gpsimd.tensor_tensor(out=result[g][:], in0=base_sb[:, g, :], in1=neg_a[g][:], op=ALU.subtract)
+            times(neg_a_mean, neg_a_sum, inv_sum, g)
 
-        def share_term(g):
+        for g in range(G):
             nc.vector.scalar_tensor_tensor(
                 out=neg_w[g][:], in0=z2_then_tz1[g][:], scalar=column(w_scale, g), in1=ex[g][:],
                 op0=ALU.mult, op1=ALU.mult, accum_out=column(neg_w_sum, g),
             )
-
-        def row_correction(g):
-            nc.vector.tensor_scalar(
-                out=column(share_scale, g), in0=column(neg_a_sum, g), scalar1=column(neg_w_sum, g),
-                scalar2=column(inv_sum, g), op0=ALU.add, op1=ALU.mult,
+            nc.scalar.activation(
+                out=column(share_scale, g), in_=column(neg_w_sum, g), func=ACT.Identity,
+                scale=column(inv_sum, g), bias=column(neg_a_mean, g),
             )
 
-        def subtract(g, minuend, term, cols):
-            nc.vector.tensor_tensor(out=result[g][:, cols], in0=minuend, in1=term[g][:, cols], op=ALU.subtract)
+        def subtract_w(g, cols):
+            nc.vector.tensor_tensor(
+                out=result[g][:, cols], in0=result[g][:, cols], in1=neg_w[g][:, cols], op=ALU.subtract
+            )
 
         def finish(g, cols):
             nc.vector.scalar_tensor_tensor(
@@ -198,18 +207,10 @@ def tile_rows_hvrowlog_kernel(tc, x, w1, w2, tp, wo, dy, dx, og, base, out):
             nc.sync.dma_start(out=out[g, :, cols], in_=result[g][:, cols])
 
         whole = slice(0, N)
-        halves = [slice(0, N // 2), slice(N // 2, N)]
-        gate_term(0)
-        share_term(0)
-        gate_term(1)
-        subtract(0, base_sb[:, 0, :], neg_a, whole)
-        share_term(1)
-        row_correction(0)
-        subtract(0, result[0][:], neg_w, whole)
-        subtract(1, base_sb[:, 1, :], neg_a, whole)
+        left, right = slice(0, N // 2), slice(N // 2, N)
+        subtract_w(0, whole)
+        subtract_w(1, left)
         finish(0, whole)
-        row_correction(1)
-        for cols in halves:
-            subtract(1, result[1][:, cols], neg_w, cols)
-        for cols in halves:
-            finish(1, cols)
+        subtract_w(1, right)
+        finish(1, left)
+        finish(1, right)

@@ -15,7 +15,7 @@ ACT = mybir.ActivationFunctionType
 P = 128
 PACK = 4
 ROWS = D // PACK
-RUN = 4
+RUN = 2
 
 FLOPS = 5 * 2 * G * D * M * N
 
@@ -41,7 +41,6 @@ def tile_rows_hvrowlog_kernel(tc, x, w1, w2, tp, wo, dy, dx, og, base, out):
                 "packed": sb.tile([P, width, PACK], BF16, name=name + "packed", align_bytes=64),
                 "codes": sb.tile([P, width], U32, name=name + "codes", align_bytes=64),
                 "scales": sb.tile([P, width], U8, name=name + "scales", align_bytes=64),
-                "width": width,
             }
 
         def interleave(copy, operand, first, last):
@@ -50,11 +49,11 @@ def tile_rows_hvrowlog_kernel(tc, x, w1, w2, tp, wo, dy, dx, og, base, out):
                 in_=operand["raw"][:, :, first:last].rearrange("p j (c i) -> p c j i", i=RUN),
             )
 
-        def quantise(operand):
+        def quantise(operand, first, last):
             nc.vector.quantize_mx(
-                out=operand["codes"][:].bitcast(FP8X4),
-                scales=operand["scales"][:],
-                in_=operand["packed"][:].rearrange("p c j -> p (c j)"),
+                out=operand["codes"][:, first:last].bitcast(FP8X4),
+                scales=operand["scales"][:, first:last],
+                in_=operand["packed"][:, first:last, :].rearrange("p c j -> p (c j)"),
             )
 
         def product(bank, weights, moving):
@@ -123,22 +122,24 @@ def tile_rows_hvrowlog_kernel(tc, x, w1, w2, tp, wo, dy, dx, og, base, out):
         interleave(on_vector, xq, 0, X_VECTOR_COLS)
         interleave(on_scalar, xq, X_VECTOR_COLS, N)
         interleave(on_vector, w2q, 0, M)
-        quantise(xq)
-        quantise(w2q)
+        quantise(xq, 0, N)
+        quantise(w2q, 0, M)
         product(z2_then_tz1, w2q, xq)
 
-        interleave(on_vector, dyq, 0, DY_VECTOR_COLS)
+        interleave(on_vector, dyq, 0, N // 2)
+        interleave(on_vector, dyq, N // 2, DY_VECTOR_COLS)
         interleave(on_scalar, dyq, DY_VECTOR_COLS, N)
         interleave(on_scalar, woq, 0, M)
-        quantise(woq)
-        quantise(dyq)
+        quantise(dyq, 0, N // 2)
+        quantise(woq, 0, M)
+        quantise(dyq, N // 2, N)
         product(c0, woq, dyq)
 
         for g in range(G):
             nc.scalar.activation(out=th[g][:], in_=z2_then_tz1[g][:], func=ACT.Tanh, scale=0.5)
 
         interleave(on_vector, w1q, 0, M)
-        quantise(w1q)
+        quantise(w1q, 0, M)
         product(z1, w1q, xq)
 
         interleave(on_scalar, dxq, DX_VECTOR_COLS, N)
@@ -160,7 +161,7 @@ def tile_rows_hvrowlog_kernel(tc, x, w1, w2, tp, wo, dy, dx, og, base, out):
             )
 
         finish_gate(0)
-        quantise(dxq)
+        quantise(dxq, 0, N)
         product(tz2, w2q, dxq)
         product(z2_then_tz1, w1q, dxq)
         nc.vector.scalar_tensor_tensor(
@@ -181,8 +182,8 @@ def tile_rows_hvrowlog_kernel(tc, x, w1, w2, tp, wo, dy, dx, og, base, out):
                 out=neg_a[g][:], in0=tz2[g][:], scalar=column(quarter_k, g), in1=gate[g][:],
                 op0=ALU.mult, op1=ALU.mult, accum_out=column(neg_a_sum, g),
             )
-            nc.gpsimd.tensor_tensor(out=result[g][:], in0=base_sb[:, g, :], in1=neg_a[g][:], op=ALU.subtract)
             times(neg_a_mean, neg_a_sum, inv_sum, g)
+        nc.gpsimd.tensor_tensor(out=result[0][:], in0=base_sb[:, 0, :], in1=neg_a[0][:], op=ALU.subtract)
 
         for g in range(G):
             nc.vector.scalar_tensor_tensor(
@@ -209,8 +210,9 @@ def tile_rows_hvrowlog_kernel(tc, x, w1, w2, tp, wo, dy, dx, og, base, out):
         whole = slice(0, N)
         left, right = slice(0, N // 2), slice(N // 2, N)
         subtract_w(0, whole)
-        subtract_w(1, left)
+        nc.vector.tensor_tensor(out=result[1][:], in0=base_sb[:, 1, :], in1=neg_a[1][:], op=ALU.subtract)
         finish(0, whole)
+        subtract_w(1, left)
         subtract_w(1, right)
         finish(1, left)
         finish(1, right)

@@ -21,7 +21,6 @@ FLOPS = 5 * 2 * G * D * M * N
 
 X_VECTOR_COLS = 344
 DY_VECTOR_COLS = 400
-DX_VECTOR_COLS = 152
 
 
 def tile_rows_hvrowlog_kernel(tc, x, w1, w2, tp, wo, dy, dx, og, base, out):
@@ -32,21 +31,28 @@ def tile_rows_hvrowlog_kernel(tc, x, w1, w2, tp, wo, dy, dx, og, base, out):
         ps = ctx.enter_context(tc.psum_pool(name="ps", bufs=1))
         ctx.enter_context(tc.manual_schedule())
 
-        def load_operand(name, src):
+        def load_operand(name, src, parts=1):
             width = src.shape[2]
-            raw = sb.tile([P, PACK, width], F32, name=name + "raw", align_bytes=64)
-            nc.sync.dma_start(out=raw[:], in_=src.rearrange("g (p j) c -> (g p) j c", j=PACK))
+            step = width // parts
+            rows = src.rearrange("g (p j) c -> (g p) j c", j=PACK)
+            raw = []
+            for part in range(parts):
+                piece = sb.tile([P, PACK, step], F32, name="%sraw%d" % (name, part), align_bytes=64)
+                nc.sync.dma_start(out=piece[:], in_=rows[:, :, part * step : (part + 1) * step])
+                raw.append(piece)
             return {
                 "raw": raw,
+                "step": step,
                 "packed": sb.tile([P, width, PACK], BF16, name=name + "packed", align_bytes=64),
                 "codes": sb.tile([P, width], U32, name=name + "codes", align_bytes=64),
                 "scales": sb.tile([P, width], U8, name=name + "scales", align_bytes=64),
             }
 
         def interleave(copy, operand, first, last):
+            part, start = divmod(first, operand["step"])
             copy(
                 out=operand["packed"][:, first:last, :].rearrange("p (c i) j -> p c j i", i=RUN),
-                in_=operand["raw"][:, :, first:last].rearrange("p j (c i) -> p c j i", i=RUN),
+                in_=operand["raw"][part][:, :, start : start + last - first].rearrange("p j (c i) -> p c j i", i=RUN),
             )
 
         def quantise(operand, first, last):
@@ -83,7 +89,7 @@ def tile_rows_hvrowlog_kernel(tc, x, w1, w2, tp, wo, dy, dx, og, base, out):
         dyq = load_operand("dy", dy)
         woq = load_operand("wo", wo)
         w1q = load_operand("w1", w1)
-        dxq = load_operand("dx", dx)
+        dxq = load_operand("dx", dx, parts=2)
         temper = sb.tile([P, G], F32)
         gain = sb.tile([P, G], F32)
         with nc.allow_non_contiguous_dma(reason="one value per feature, features on partitions"):
@@ -142,7 +148,8 @@ def tile_rows_hvrowlog_kernel(tc, x, w1, w2, tp, wo, dy, dx, og, base, out):
         quantise(w1q, 0, M)
         product(z1, w1q, xq)
 
-        interleave(on_scalar, dxq, DX_VECTOR_COLS, N)
+        interleave(on_scalar, dxq, 0, N // 2)
+        interleave(on_scalar, dxq, N // 2, N)
         for g in range(G):
             nc.scalar.activation(
                 out=ex[g][:], in_=z1[g][:], func=ACT.Exp, scale=column(temper, g), accum_out=column(exp_sum, g)
@@ -153,15 +160,15 @@ def tile_rows_hvrowlog_kernel(tc, x, w1, w2, tp, wo, dy, dx, og, base, out):
                 out=gate[g][:], in0=th[g][:], scalar=1.0, in1=c0[g][:], op0=ALU.add, op1=ALU.mult,
                 accum_out=column(gate_sum, g),
             )
-        interleave(on_vector, dxq, 0, DX_VECTOR_COLS)
 
         def finish_gate(g):
             nc.vector.scalar_tensor_tensor(
                 out=gate[g][:], in0=th[g][:], scalar=1.0, in1=gate[g][:], op0=ALU.subtract, op1=ALU.mult
             )
 
+        quantise(dxq, 0, N // 2)
         finish_gate(0)
-        quantise(dxq, 0, N)
+        quantise(dxq, N // 2, N)
         product(tz2, w2q, dxq)
         product(z2_then_tz1, w1q, dxq)
         nc.vector.scalar_tensor_tensor(
@@ -171,17 +178,21 @@ def tile_rows_hvrowlog_kernel(tc, x, w1, w2, tp, wo, dy, dx, og, base, out):
         nc.vector.scalar_tensor_tensor(
             out=half_k_temper[:], in0=quarter_k[:], scalar=2.0, in1=temper[:], op0=ALU.mult, op1=ALU.mult
         )
-        nc.vector.reciprocal(out=inv_sum[:], in_=exp_sum[:])
         for g in range(G):
             times(scaled_gate_sum, gate_sum, half_k_temper, g)
-        for g in range(G):
-            times(w_scale, scaled_gate_sum, inv_sum, g)
 
-        for g in range(G):
+        def gate_term(g):
             nc.vector.scalar_tensor_tensor(
                 out=neg_a[g][:], in0=tz2[g][:], scalar=column(quarter_k, g), in1=gate[g][:],
                 op0=ALU.mult, op1=ALU.mult, accum_out=column(neg_a_sum, g),
             )
+
+        gate_term(0)
+        nc.vector.reciprocal(out=inv_sum[:], in_=exp_sum[:])
+        gate_term(1)
+        for g in range(G):
+            times(w_scale, scaled_gate_sum, inv_sum, g)
+        for g in range(G):
             times(neg_a_mean, neg_a_sum, inv_sum, g)
         nc.gpsimd.tensor_tensor(out=result[0][:], in0=base_sb[:, 0, :], in1=neg_a[0][:], op=ALU.subtract)
 

@@ -20,7 +20,9 @@ RUN = 2
 FLOPS = 5 * 2 * G * D * M * N
 
 X_VECTOR_COLS = 344
-DY_VECTOR_COLS = 400
+DY_VECTOR_COLS = 424
+GPSIMD_COLS = 128
+DX_SCALAR_COLS = 464
 
 
 def tile_rows_hvrowlog_kernel(tc, x, w1, w2, tp, wo, dy, dx, og, base, out):
@@ -31,17 +33,19 @@ def tile_rows_hvrowlog_kernel(tc, x, w1, w2, tp, wo, dy, dx, og, base, out):
         ps = ctx.enter_context(tc.psum_pool(name="ps", bufs=1))
         ctx.enter_context(tc.manual_schedule())
 
-        def load_operand(name, src, parts=1):
+        def load(operand, part):
+            step = operand["step"]
+            nc.sync.dma_start(out=operand["raw"][part][:], in_=operand["rows"][:, :, part * step : (part + 1) * step])
+
+        def make_operand(name, src, parts):
             width = src.shape[2]
             step = width // parts
-            rows = src.rearrange("g (p j) c -> (g p) j c", j=PACK)
-            raw = []
-            for part in range(parts):
-                piece = sb.tile([P, PACK, step], F32, name="%sraw%d" % (name, part), align_bytes=64)
-                nc.sync.dma_start(out=piece[:], in_=rows[:, :, part * step : (part + 1) * step])
-                raw.append(piece)
             return {
-                "raw": raw,
+                "rows": src.rearrange("g (p j) c -> (g p) j c", j=PACK),
+                "raw": [
+                    sb.tile([P, PACK, step], F32, name="%sraw%d" % (name, part), align_bytes=64)
+                    for part in range(parts)
+                ],
                 "step": step,
                 "packed": sb.tile([P, width, PACK], BF16, name=name + "packed", align_bytes=64),
                 "codes": sb.tile([P, width], U32, name=name + "codes", align_bytes=64),
@@ -84,12 +88,20 @@ def tile_rows_hvrowlog_kernel(tc, x, w1, w2, tp, wo, dy, dx, og, base, out):
         on_vector = nc.vector.tensor_copy
         on_scalar = nc.scalar.copy
 
-        xq = load_operand("x", x)
-        w2q = load_operand("w2", w2)
-        dyq = load_operand("dy", dy)
-        woq = load_operand("wo", wo)
-        w1q = load_operand("w1", w1)
-        dxq = load_operand("dx", dx, parts=2)
+        xq = make_operand("x", x, 1)
+        w2q = make_operand("w2", w2, 1)
+        dyq = make_operand("dy", dy, 2)
+        woq = make_operand("wo", wo, 1)
+        w1q = make_operand("w1", w1, 1)
+        dxq = make_operand("dx", dx, 2)
+        load(xq, 0)
+        load(w2q, 0)
+        load(dyq, 0)
+        load(woq, 0)
+        load(dyq, 1)
+        load(w1q, 0)
+        load(dxq, 0)
+        load(dxq, 1)
         temper = sb.tile([P, G], F32)
         gain = sb.tile([P, G], F32)
         with nc.allow_non_contiguous_dma(reason="one value per feature, features on partitions"):
@@ -132,24 +144,26 @@ def tile_rows_hvrowlog_kernel(tc, x, w1, w2, tp, wo, dy, dx, og, base, out):
         quantise(w2q, 0, M)
         product(z2_then_tz1, w2q, xq)
 
+        def half_tanh(g):
+            nc.scalar.activation(out=th[g][:], in_=z2_then_tz1[g][:], func=ACT.Tanh, scale=0.5)
+
         interleave(on_vector, dyq, 0, N // 2)
-        interleave(on_vector, dyq, N // 2, DY_VECTOR_COLS)
-        interleave(on_scalar, dyq, DY_VECTOR_COLS, N)
         interleave(on_scalar, woq, 0, M)
         quantise(dyq, 0, N // 2)
+        interleave(on_vector, dyq, N // 2, DY_VECTOR_COLS)
+        interleave(on_scalar, dyq, DY_VECTOR_COLS, N)
         quantise(woq, 0, M)
         quantise(dyq, N // 2, N)
         product(c0, woq, dyq)
-
         for g in range(G):
-            nc.scalar.activation(out=th[g][:], in_=z2_then_tz1[g][:], func=ACT.Tanh, scale=0.5)
+            half_tanh(g)
 
         interleave(on_vector, w1q, 0, M)
         quantise(w1q, 0, M)
         product(z1, w1q, xq)
 
         interleave(on_scalar, dxq, 0, N // 2)
-        interleave(on_scalar, dxq, N // 2, N)
+        interleave(on_scalar, dxq, N // 2, DX_SCALAR_COLS)
         for g in range(G):
             nc.scalar.activation(
                 out=ex[g][:], in_=z1[g][:], func=ACT.Exp, scale=column(temper, g), accum_out=column(exp_sum, g)
@@ -167,6 +181,7 @@ def tile_rows_hvrowlog_kernel(tc, x, w1, w2, tp, wo, dy, dx, og, base, out):
             )
 
         quantise(dxq, 0, N // 2)
+        interleave(on_vector, dxq, DX_SCALAR_COLS, N)
         finish_gate(0)
         quantise(dxq, N // 2, N)
         product(tz2, w2q, dxq)
@@ -195,6 +210,10 @@ def tile_rows_hvrowlog_kernel(tc, x, w1, w2, tp, wo, dy, dx, og, base, out):
         for g in range(G):
             times(neg_a_mean, neg_a_sum, inv_sum, g)
         nc.gpsimd.tensor_tensor(out=result[0][:], in0=base_sb[:, 0, :], in1=neg_a[0][:], op=ALU.subtract)
+        nc.gpsimd.tensor_tensor(
+            out=result[1][:, :GPSIMD_COLS], in0=base_sb[:, 1, :GPSIMD_COLS], in1=neg_a[1][:, :GPSIMD_COLS],
+            op=ALU.subtract,
+        )
 
         for g in range(G):
             nc.vector.scalar_tensor_tensor(
@@ -221,7 +240,10 @@ def tile_rows_hvrowlog_kernel(tc, x, w1, w2, tp, wo, dy, dx, og, base, out):
         whole = slice(0, N)
         left, right = slice(0, N // 2), slice(N // 2, N)
         subtract_w(0, whole)
-        nc.vector.tensor_tensor(out=result[1][:], in0=base_sb[:, 1, :], in1=neg_a[1][:], op=ALU.subtract)
+        nc.vector.tensor_tensor(
+            out=result[1][:, GPSIMD_COLS:], in0=base_sb[:, 1, GPSIMD_COLS:], in1=neg_a[1][:, GPSIMD_COLS:],
+            op=ALU.subtract,
+        )
         finish(0, whole)
         subtract_w(1, left)
         subtract_w(1, right)

from contextlib import ExitStack

import concourse.mybir as mybir

G, D, M, N = 2, 256, 128, 512

F32 = mybir.dt.float32
BF16 = mybir.dt.bfloat16
U32 = mybir.dt.uint32
U8 = mybir.dt.uint8
FP8X4 = mybir.dt.float8_e4m3fn_x4
ALU = mybir.AluOpType
ACT = mybir.ActivationFunctionType

P = 128
PACK = 4
ROWS = D // PACK
RUN = 2

FLOPS = 5 * 2 * G * D * M * N

X_VECTOR_COLS = 344
DY_VECTOR_COLS = 424
GPSIMD_COLS = 128
DX_SCALAR_COLS = 464


def tile_rows_hvrowlog_kernel(tc, x, w1, w2, tp, wo, dy, dx, og, base, out):
    nc = tc.nc

    with ExitStack() as ctx:
        sb = ctx.enter_context(tc.tile_pool(name="sb", bufs=1))
        ps = ctx.enter_context(tc.psum_pool(name="ps", bufs=1))
        ctx.enter_context(tc.manual_schedule())

        def load(operand, part):
            step = operand["step"]
            nc.sync.dma_start(out=operand["raw"][part][:], in_=operand["rows"][:, :, part * step : (part + 1) * step])

        def make_operand(name, src, parts):
            width = src.shape[2]
            step = width // parts
            return {
                "rows": src.rearrange("g (p j) c -> (g p) j c", j=PACK),
                "raw": [
                    sb.tile([P, PACK, step], F32, name="%sraw%d" % (name, part), align_bytes=64)
                    for part in range(parts)
                ],
                "step": step,
                "packed": sb.tile([P, width, PACK], BF16, name=name + "packed", align_bytes=64),
                "codes": sb.tile([P, width], U32, name=name + "codes", align_bytes=64),
                "scales": sb.tile([P, width], U8, name=name + "scales", align_bytes=64),
            }

        def interleave(copy, operand, first, last):
            part, start = divmod(first, operand["step"])
            copy(
                out=operand["packed"][:, first:last, :].rearrange("p (c i) j -> p c j i", i=RUN),
                in_=operand["raw"][part][:, :, start : start + last - first].rearrange("p j (c i) -> p c j i", i=RUN),
            )

        def quantise(operand, first, last):
            nc.vector.quantize_mx(
                out=operand["codes"][:, first:last].bitcast(FP8X4),
                scales=operand["scales"][:, first:last],
                in_=operand["packed"][:, first:last, :].rearrange("p c j -> p (c j)"),
            )

        def product(bank, weights, moving):
            for g in range(G):
                rows = slice(ROWS * g, ROWS * (g + 1))
                nc.tensor.matmul_mx(
                    out=bank[g][:],
                    lhsT=weights["codes"][rows, :].bitcast(FP8X4),
                    lhsT_scale=weights["scales"][rows, :],
                    rhs=moving["codes"][rows, :].bitcast(FP8X4),
                    rhs_scale=moving["scales"][rows, :],
                    start=True,
                    stop=True,
                )

        def per_group(pool, name, width):
            return [pool.tile([P, width], F32, name="%s%d" % (name, g)) for g in range(G)]

        def column(stat, g):
            return stat[:, g : g + 1]

        on_vector = nc.vector.tensor_copy
        on_scalar = nc.scalar.copy

        xq = make_operand("x", x, 1)
        w2q = make_operand("w2", w2, 1)
        dyq = make_operand("dy", dy, 2)
        woq = make_operand("wo", wo, 1)
        w1q = make_operand("w1", w1, 1)
        dxq = make_operand("dx", dx, 2)
        load(xq, 0)
        load(w2q, 0)
        load(dyq, 0)
        load(woq, 0)
        load(dyq, 1)
        load(w1q, 0)
        load(dxq, 0)
        load(dxq, 1)
        temper = sb.tile([P, G], F32)
        gain = sb.tile([P, G], F32)
        with nc.allow_non_contiguous_dma(reason="one value per feature, features on partitions"):
            nc.sync.dma_start(out=temper[:], in_=tp.rearrange("g m o -> m (g o)"))
            nc.sync.dma_start(out=gain[:], in_=og.rearrange("g m o -> m (g o)"))
        base_sb = sb.tile([P, G, N], F32)
        nc.sync.dma_start(out=base_sb[:], in_=base.rearrange("g m n -> m g n"))

        z2_then_tz1 = per_group(ps, "bank_a", N)
        z1 = per_group(ps, "bank_b", N)
        c0 = per_group(ps, "bank_c", N)
        tz2 = per_group(ps, "bank_d", N)

        th = per_group(sb, "th", N)
        ex = per_group(sb, "ex", N)
        gate = per_group(sb, "gate", N)
        neg_a = per_group(sb, "neg_a", N)
        neg_w = per_group(sb, "neg_w", N)
        result = per_group(sb, "result", N)

        quarter_k = sb.tile([P, G], F32)
        half_k_temper = sb.tile([P, G], F32)
        exp_sum = sb.tile([P, G], F32)
        inv_sum = sb.tile([P, G], F32)
        gate_sum = sb.tile([P, G], F32)
        scaled_gate_sum = sb.tile([P, G], F32)
        w_scale = sb.tile([P, G], F32)
        neg_a_sum = sb.tile([P, G], F32)
        neg_a_mean = sb.tile([P, G], F32)
        neg_w_sum = sb.tile([P, G], F32)
        share_scale = sb.tile([P, G], F32)

        def times(dst, src, factor, g):
            nc.scalar.activation(out=column(dst, g), in_=column(src, g), func=ACT.Copy, scale=column(factor, g))

        interleave(on_vector, xq, 0, X_VECTOR_COLS)
        interleave(on_scalar, xq, X_VECTOR_COLS, N)
        interleave(on_vector, w2q, 0, M)
        quantise(xq, 0, N)
        quantise(w2q, 0, M)
        product(z2_then_tz1, w2q, xq)

        def half_tanh(g):
            nc.scalar.activation(out=th[g][:], in_=z2_then_tz1[g][:], func=ACT.Tanh, scale=0.5)

        interleave(on_vector, dyq, 0, N // 2)
        interleave(on_scalar, woq, 0, M)
        quantise(dyq, 0, N // 2)
        interleave(on_vector, dyq, N // 2, DY_VECTOR_COLS)
        interleave(on_scalar, dyq, DY_VECTOR_COLS, N)
        quantise(woq, 0, M)
        quantise(dyq, N // 2, N)
        product(c0, woq, dyq)
        for g in range(G):
            half_tanh(g)

        interleave(on_vector, w1q, 0, M)
        quantise(w1q, 0, M)
        product(z1, w1q, xq)

        interleave(on_scalar, dxq, 0, N // 2)
        interleave(on_scalar, dxq, N // 2, DX_SCALAR_COLS)
        for g in range(G):
            nc.scalar.activation(
                out=ex[g][:], in_=z1[g][:], func=ACT.Exp, scale=column(temper, g), accum_out=column(exp_sum, g)
            )

        for g in range(G):
            nc.vector.scalar_tensor_tensor(
                out=gate[g][:], in0=th[g][:], scalar=1.0, in1=c0[g][:], op0=ALU.add, op1=ALU.mult,
                accum_out=column(gate_sum, g),
            )

        def finish_gate(g):
            nc.vector.scalar_tensor_tensor(
                out=gate[g][:], in0=th[g][:], scalar=1.0, in1=gate[g][:], op0=ALU.subtract, op1=ALU.mult
            )

        quantise(dxq, 0, N // 2)
        interleave(on_vector, dxq, DX_SCALAR_COLS, N)
        finish_gate(0)
        quantise(dxq, N // 2, N)
        product(tz2, w2q, dxq)
        product(z2_then_tz1, w1q, dxq)
        nc.vector.scalar_tensor_tensor(
            out=quarter_k[:], in0=temper[:], scalar=0.25, in1=gain[:], op0=ALU.mult, op1=ALU.mult
        )
        finish_gate(1)
        nc.vector.scalar_tensor_tensor(
            out=half_k_temper[:], in0=quarter_k[:], scalar=2.0, in1=temper[:], op0=ALU.mult, op1=ALU.mult
        )
        for g in range(G):
            times(scaled_gate_sum, gate_sum, half_k_temper, g)

        def gate_term(g):
            nc.vector.scalar_tensor_tensor(
                out=neg_a[g][:], in0=tz2[g][:], scalar=column(quarter_k, g), in1=gate[g][:],
                op0=ALU.mult, op1=ALU.mult, accum_out=column(neg_a_sum, g),
            )

        gate_term(0)
        nc.vector.reciprocal(out=inv_sum[:], in_=exp_sum[:])
        gate_term(1)
        for g in range(G):
            times(w_scale, scaled_gate_sum, inv_sum, g)
        for g in range(G):
            times(neg_a_mean, neg_a_sum, inv_sum, g)
        nc.gpsimd.tensor_tensor(out=result[0][:], in0=base_sb[:, 0, :], in1=neg_a[0][:], op=ALU.subtract)
        nc.gpsimd.tensor_tensor(
            out=result[1][:, :GPSIMD_COLS], in0=base_sb[:, 1, :GPSIMD_COLS], in1=neg_a[1][:, :GPSIMD_COLS],
            op=ALU.subtract,
        )

        for g in range(G):
            nc.vector.scalar_tensor_tensor(
                out=neg_w[g][:], in0=z2_then_tz1[g][:], scalar=column(w_scale, g), in1=ex[g][:],
                op0=ALU.mult, op1=ALU.mult, accum_out=column(neg_w_sum, g),
            )
            nc.scalar.activation(
                out=column(share_scale, g), in_=column(neg_w_sum, g), func=ACT.Identity,
                scale=column(inv_sum, g), bias=column(neg_a_mean, g),
            )

        def subtract_w(g, cols):
            nc.vector.tensor_tensor(
                out=result[g][:, cols], in0=result[g][:, cols], in1=neg_w[g][:, cols], op=ALU.subtract
            )

        def finish(g, cols):
            nc.vector.scalar_tensor_tensor(
                out=result[g][:, cols], in0=ex[g][:, cols], scalar=column(share_scale, g), in1=result[g][:, cols],
                op0=ALU.mult, op1=ALU.add,
            )
            nc.sync.dma_start(out=out[g, :, cols], in_=result[g][:, cols])

        whole = slice(0, N)
        left, right = slice(0, N // 2), slice(N // 2, N)
        subtract_w(0, whole)
        nc.vector.tensor_tensor(
            out=result[1][:, GPSIMD_COLS:], in0=base_sb[:, 1, GPSIMD_COLS:], in1=neg_a[1][:, GPSIMD_COLS:],
            op=ALU.subtract,
        )
        finish(0, whole)
        subtract_w(1, left)
        subtract_w(1, right)
        finish(1, left)
        finish(1, right)
